import numpy as np
import ml_dtypes


def mxq(x, axis, fmt="e4m3"):
    dtype, down = {"e4m3": (ml_dtypes.float8_e4m3fn, 7), "e5m2": (ml_dtypes.float8_e5m2, 14)}[fmt]
    v = np.moveaxis(np.asarray(x, np.float32).astype(ml_dtypes.bfloat16).astype(np.float64), axis, -1)
    blocks = v.reshape(v.shape[:-1] + (-1, 32))
    amax = np.abs(blocks).max(-1, keepdims=True)
    byte = np.maximum(np.where(amax > 0, np.frexp(amax)[1] - 1 + 127, 0) - down, 1)
    scale = np.exp2(byte - 127.0)
    codes = (blocks / scale).astype(np.float32).astype(dtype).astype(np.float64)
    return np.moveaxis((codes * scale).reshape(v.shape), -1, axis)


WIDE = False


def mx_kscale(k):
    if not WIDE:
        return np.ones(k)
    levels = np.array([10, -10, 5, -5, 0])
    if k % 512:
        return np.exp2(np.random.permutation(np.resize(levels, k // 32))).repeat(32)
    a = np.empty((k // 512, 16))
    for p in range(k // 512):
        a[p, :8] = np.random.permutation(np.resize(levels, 8))
        for g in range(8):
            far = levels[np.abs(levels - a[p, g]) >= 10]
            a[p, g + 8] = far[np.random.randint(len(far))]
    return np.exp2(a.ravel()).repeat(32)


BF16 = ml_dtypes.bfloat16


def bf(x):
    return np.asarray(x, np.float32).astype(BF16)


def f64(x):
    return np.asarray(x).astype(np.float64)


E2M1 = np.array([0.0, 0.5, 1.0, 1.5, 2.0, 3.0, 4.0, 6.0, -0.0, -0.5, -1.0, -1.5, -2.0, -3.0, -4.0, -6.0])


def pack_weight(w, fmt):
    k, n = w.shape
    w = f64(bf(w)).reshape(k // 32, 32, n)
    amax = np.abs(w).max(1)
    if fmt == "e4m3":
        byte = np.frexp(amax)[1] - 1 + 127 - 7
    else:
        mant, ex = np.frexp(amax / 6.0)
        byte = np.where(mant > 0.5, ex, ex - 1) + 127
    byte = np.clip(np.where(amax > 0, byte, 1), 1, 254)
    scaled = (w * np.exp2(127.0 - byte)[:, None, :]).reshape(k, n).astype(np.float32)
    by_word = np.ascontiguousarray(scaled.reshape(k // 512, 128, 4, n).transpose(0, 1, 3, 2))
    if fmt == "e4m3":
        words = by_word.astype(ml_dtypes.float8_e4m3fn).view(np.uint8)
    else:
        c = by_word.astype(ml_dtypes.float4_e2m1fn).view(np.uint8) & 0xF
        words = c[..., 0::2] | (c[..., 1::2] << 4)
    return np.ascontiguousarray(words), np.ascontiguousarray(byte.astype(np.uint8).reshape(k // 512, 16, n))


def unpack_weight(words, scales, fmt):
    g, p, n, _ = words.shape
    if fmt == "e4m3":
        vals = np.ascontiguousarray(words).view(ml_dtypes.float8_e4m3fn).astype(np.float64)
    else:
        nib = np.empty((g, p, n, 4), np.uint8)
        nib[..., 0::2] = words & 0xF
        nib[..., 1::2] = words >> 4
        vals = E2M1[nib]
    vals = vals * np.repeat(np.exp2(scales.astype(np.float64) - 127.0), 8, axis=1)[..., None]
    return vals.transpose(0, 1, 3, 2).reshape(g * 512, n)
def pack4(w):
    words, scales = pack_weight(w, "e2m1")
    return words.reshape(words.shape[0], 128, -1), scales


def unpack4(words, scales):
    return unpack_weight(words.reshape(words.shape[0], 128, -1, 2), scales, "e2m1")


M, H, D, N = 1024, 2, 512, 2048


def sigmoid(a):
    return 1.0 / (1.0 + np.exp(-a))


def draw0():
    r = mx_kscale(H * D)
    t = mx_kscale(H * N)
    km = np.random.standard_normal((H * D, N)) / np.sqrt(D) / r[:, None]
    vm = 4.0 * np.random.standard_normal((H * N, D)) / t[:, None]
    k_words, k_scales = pack4(km)
    v_words, v_scales = pack4(vm)
    distance = np.abs(np.arange(M)[:, None] / M - np.arange(N)[None, :] / N)
    return {"x": bf(1.5 * np.random.standard_normal((M, H * D)) * r),
            "k_words": k_words,
            "k_scales": k_scales,
            "v_words": v_words,
            "v_scales": v_scales,
            "bias": bf(0.5 * np.random.standard_normal((M, N)) - 4.0 * distance),
            "slopes": bf(2.0 ** (-np.arange(H)) * (1.0 + 0.1 * np.random.standard_normal(H))),
            "slot_gain": bf((1.0 + 0.1 * np.random.standard_normal((H, N))) * t.reshape(H, N)),
            "gate": bf(np.random.standard_normal((M, H * D)))}


def core(x, k_words, k_scales, v_words, v_scales, bias, slopes, slot_gain, gate):
    xq = mxq(f64(x), 1, "e4m3")
    km = unpack4(k_words, k_scales)
    vm = unpack4(v_words, v_scales)
    b, sl, sg = f64(bias), f64(slopes), f64(slot_gain)
    heads = []
    for h in range(H):
        score = xq[:, h * D:(h + 1) * D] @ km[h * D:(h + 1) * D]
        score = score + sl[h] * b
        e = np.exp(score - np.max(score, axis=1, keepdims=True))
        total = np.sum(e, axis=1, keepdims=True)
        y = mxq(e * sg[h], 1, "e4m3") @ vm[h * N:(h + 1) * N]
        heads.append(y / total)
    return np.concatenate(heads, axis=1) * sigmoid(f64(gate))


def e4m3fn_bytes(y):
    return np.clip(np.asarray(y, np.float64), -448.0, 448.0).astype(np.float32).astype(ml_dtypes.float8_e4m3fn).view(np.uint8)


def e4m3fn_values(b):
    return np.asarray(b, np.uint8).view(ml_dtypes.float8_e4m3fn).astype(np.float64)


def setup_inputs():
    d = draw0()
    x0 = np.asarray(d['x']).astype(np.float64)
    s = (np.max(np.abs(x0), axis=(0,), keepdims=True) / 448.0).astype(np.float32)
    out = {}
    for k, v in d.items():
        if k == 'x':
            out['x_bytes'] = e4m3fn_bytes(x0 / s.astype(np.float64))
            out['x_scale'] = s
        else:
            out[k] = v
    return out


def reference(x_bytes, x_scale, k_words, k_scales, v_words, v_scales, bias, slopes, slot_gain, gate):
    return core(e4m3fn_values(x_bytes) * x_scale.astype(np.float64), k_words, k_scales, v_words, v_scales, bias, slopes, slot_gain, gate)

@@ -1,0 +1,414 @@
+from contextlib import ExitStack
+
+import concourse.mybir as mybir
+from concourse.masks import make_identity
+
+F32 = mybir.dt.float32
+BF16 = mybir.dt.bfloat16
+I32 = mybir.dt.int32
+U32 = mybir.dt.uint32
+U8 = mybir.dt.uint8
+FP8 = mybir.dt.float8_e4m3fn
+FP8X4 = mybir.dt.float8_e4m3fn_x4
+FP4X4 = mybir.dt.float4_e2m1fn_x4
+ACT = mybir.ActivationFunctionType
+ALU = mybir.AluOpType
+AX = mybir.AxisListType
+
+M, H, D, N = 1024, 2, 512, 2048
+P = 128
+QT = M // P
+TILES = QT * H
+CH = 512
+NCH = N // CH
+
+FLOPS = 2 * 2 * H * M * D * N
+
+
+def tile_alibi_slot_attention_f1_kernel(
+    tc, x_bytes, x_scale, k_words, k_scales, v_words, v_scales, bias, slopes, slot_gain, gate, out
+):
+    nc = tc.nc
+    with ExitStack() as ctx:
+        keep = ctx.enter_context(tc.tile_pool(name="keep", bufs=1))
+        work = ctx.enter_context(tc.tile_pool(name="work", bufs=2))
+        sc_pool = ctx.enter_context(tc.psum_pool(name="sc_pool", bufs=4))
+        tp_pool = ctx.enter_context(tc.psum_pool(name="tp_pool", bufs=2))
+        pv_pool = ctx.enter_context(tc.psum_pool(name="pv_pool", bufs=1))
+        xt_pool = ctx.enter_context(tc.psum_pool(name="xt_pool", bufs=1))
+        ctx.enter_context(tc.manual_schedule())
+
+        xb = keep.tile([P, QT, H * D], U8, name="xb", align_bytes=64)
+        xsc = keep.tile([P, H * D], F32, name="xsc")
+        kw = keep.tile([P, H, 2 * N], U8, name="kw", align_bytes=64)
+        ksc = keep.tile([P, H, N], U8, name="ksc", align_bytes=64)
+        vw = keep.tile([P, H * NCH, 2 * D], U8, name="vw", align_bytes=64)
+        vsc = keep.tile([P, H * NCH, D], U8, name="vsc", align_bytes=64)
+        bias_sb = keep.tile([P, QT, N], BF16, name="bias_sb")
+        gain = keep.tile([P, H, N], BF16, name="gain")
+        gate_sb = keep.tile([P, QT, H * D], BF16, name="gate_sb")
+        slope = keep.tile([P, H], BF16, name="slope")
+        nslope = keep.tile([P, H], F32, name="nslope")
+        xcodes = keep.tile([P, QT, H * P], U32, name="xcodes", align_bytes=64)
+        xqs = keep.tile([P, QT, H * P], U8, name="xqs", align_bytes=64)
+        ident = keep.tile([P, P], F32, name="ident")
+        dummy = keep.tile([P, 1], F32, name="dummy")
+        tot4 = keep.tile([P, NCH], F32, name="tot4")
+
+        nc.vector.memset(dummy[:], 0.0)
+        nc.scalar.activation(out=dummy[:], in_=dummy[:], func=ACT.Exp)
+        nc.vector.memset(ksc[:].rearrange("p g n -> p (g n)").bitcast(I32), 0)
+        make_identity(nc, ident[:])
+        nc.vector.memset(vsc[:].rearrange("p g n -> p (g n)").bitcast(I32), 0)
+
+        x_rows = x_bytes.rearrange("(j p) k -> p j k", p=P)
+        bias_rows = bias.rearrange("(j p) n -> p j n", p=P)
+        gate_rows = gate.rearrange("(j p) n -> p j n", p=P)
+        xs_row = x_scale.rearrange("o k -> (o k)")
+        ks_i32 = k_scales.bitcast(I32).rearrange("g r n -> r g n")
+        vs_i32 = v_scales.bitcast(I32).rearrange("g r n -> r g n")
+        kw_rows = k_words.rearrange("g p n -> p g n")
+        vw_rows = v_words.rearrange("g p n -> p g n")
+
+        def load(dst, src):
+            nc.sync.dma_start(out=dst, in_=src)
+
+        load(xb[:, 0:2, :], x_rows[:, 0:2, :])
+        for h in range(H):
+            load(xsc[:, h * D : (h + 1) * D], xs_row[h * D : (h + 1) * D].partition_broadcast(P))
+        for q in range(4):
+            load(ksc[32 * q : 32 * q + 4, :, :].bitcast(I32), ks_i32[4 * q : 4 * q + 4])
+        load(kw[:, 0, 0:N], kw_rows[:, 0, 0:N])
+        load(kw[:, 0, N:], kw_rows[:, 0, N:])
+        load(slope[:], slopes.partition_broadcast(P))
+        load(bias_sb[:, 0, 0 : N // 2], bias_rows[:, 0, 0 : N // 2])
+        load(bias_sb[:, 0, N // 2 :], bias_rows[:, 0, N // 2 :])
+        load(xb[:, 2:4, :], x_rows[:, 2:4, :])
+        load(kw[:, 1, :], kw_rows[:, 1, :])
+        load(gain[:, 0, :], slot_gain[0, :].partition_broadcast(P))
+        load(gate_sb[:, 0, :], gate_rows[:, 0, :])
+        load(gate_sb[:, 1, :], gate_rows[:, 1, :])
+        load(gain[:, 1, :], slot_gain[1, :].partition_broadcast(P))
+        load(bias_sb[:, 1, :], bias_rows[:, 1, :])
+        for q in range(4):
+            load(vsc[32 * q : 32 * q + 4, :, :].bitcast(I32), vs_i32[4 * q : 4 * q + 4])
+        load(vw[:, 0:4, :], vw_rows[:, 0:4, :])
+        load(bias_sb[:, 2, :], bias_rows[:, 2, :])
+        load(xb[:, 4:8, :], x_rows[:, 4:8, :])
+        load(vw[:, 4:8, :], vw_rows[:, 4:8, :])
+        load(gate_sb[:, 2:4, :], gate_rows[:, 2:4, :])
+        for j in range(3, QT):
+            load(bias_sb[:, j, :], bias_rows[:, j, :])
+            if j == 4:
+                load(gate_sb[:, 4:8, :], gate_rows[:, 4:8, :])
+
+        xw = {}
+        xs = {}
+        xt = {}
+
+        def x_tile(j):
+            xs[j] = work.tile([P, H * D], BF16, name="x_scaled", bufs=3, align_bytes=64)
+
+        def x_scale_v(j, h):
+            cols = slice(h * D, (h + 1) * D)
+            nc.vector.tensor_tensor(out=xs[j][:, cols], in0=xb[:, j, cols].bitcast(FP8), in1=xsc[:, cols], op=ALU.mult)
+
+        def x_widen(j):
+            xw[j] = work.tile([P, H * D], F32, name="x_wide")
+            nc.scalar.copy(out=xw[j][:], in_=xb[:, j, :].bitcast(FP8))
+
+        def x_scale_g(j, h):
+            if h == 0:
+                x_tile(j)
+            cols = slice(h * D, (h + 1) * D)
+            nc.gpsimd.tensor_tensor(out=xs[j][:, cols], in0=xw[j][:, cols], in1=xsc[:, cols], op=ALU.mult)
+
+        def x_turn(j):
+            words = xs[j][:].bitcast(F32)
+            xt[j] = xt_pool.tile([P, H, 2, P], F32, name="x_turned")
+            for h in range(H):
+                for u in range(2):
+                    nc.tensor.transpose(xt[j][:, h, u, :], words[:, 256 * h + u : 256 * (h + 1) : 2], ident[:])
+
+        def x_spread(j):
+            xi = work.tile([P, H, P, 4], BF16, name="x_spread", align_bytes=64)
+            nc.scalar.copy(
+                out=xi[:].rearrange("p h r t -> p (h r t)").bitcast(F32).rearrange("p (h r u) -> p h r u", h=H, u=2),
+                in_=xt[j][:].rearrange("p h u r -> p h r u"),
+            )
+            xt[j] = xi
+
+        def x_quant(j):
+            nc.vector.quantize_mx(
+                out=xcodes[:, j, :].bitcast(FP8X4), scales=xqs[:, j, :], in_=xt[j][:].rearrange("p h r t -> p (h r t)")
+            )
+
+        sg = {}
+
+        def gate_tanh(j):
+            sg[j] = work.tile([P, H * D], F32, name="sgm", bufs=5)
+            nc.scalar.activation(out=sg[j][:], in_=gate_sb[:, j, :], func=ACT.Tanh, scale=0.5)
+
+        def gate_affine(j):
+            nc.scalar.activation(out=sg[j][:], in_=sg[j][:], func=ACT.Copy, scale=0.5, bias=0.5)
+
+        sc, neg, nmx, ex, tot, aa = {}, {}, {}, {}, {}, {}
+        tp, at, cod, cos, pv, rec = {}, {}, {}, {}, {}, {}
+
+        def qk(i, c):
+            j, h = divmod(i, H)
+            sc[i, c] = sc_pool.tile([P, CH], F32, name="scores")
+            nc.tensor.matmul_mx(
+                out=sc[i, c][:],
+                lhsT=xcodes[:, j, h * P : (h + 1) * P].bitcast(FP8X4),
+                lhsT_scale=xqs[:, j, h * P : (h + 1) * P],
+                rhs=kw[:, h, 2 * CH * c : 2 * CH * (c + 1)].bitcast(FP4X4),
+                rhs_scale=ksc[:, h, CH * c : CH * (c + 1)],
+                start=True,
+                stop=True,
+            )
+
+        def add_bias(i, c):
+            j, h = divmod(i, H)
+            if c == 0:
+                neg[i] = work.tile([P, N], F32, name="neg", bufs=3)
+            cols = slice(CH * c, CH * (c + 1))
+            nc.vector.scalar_tensor_tensor(
+                out=neg[i][:, cols], in0=bias_sb[:, j, cols], scalar=nslope[:, h : h + 1], in1=sc[i, c][:],
+                op0=ALU.mult, op1=ALU.subtract,
+            )
+
+        def row_max(i):
+            nmx[i] = work.tile([P, 1], F32, name="nmx", bufs=3)
+            nc.vector.tensor_reduce(out=nmx[i][:], in_=neg[i][:], axis=AX.X, op=ALU.min)
+
+        def exps(i):
+            ex[i] = work.tile([P, N], F32, name="ex")
+            tot[i] = work.tile([P, 1], F32, name="tot", bufs=5)
+            nc.scalar.activation(
+                out=ex[i][:], in_=neg[i][:], func=ACT.Exp, bias=nmx[i][:], scale=-1.0, accum_out=tot[i][:]
+            )
+
+        def exps_piece(i, c):
+            if c == 0:
+                ex[i] = work.tile([P, N], F32, name="ex")
+            cols = slice(CH * c, CH * (c + 1))
+            nc.scalar.activation(
+                out=ex[i][:, cols], in_=neg[i][:, cols], func=ACT.Exp, bias=nmx[i][:], scale=-1.0,
+                accum_out=tot4[:, c : c + 1],
+            )
+
+        def gains(eng, i, c):
+            h = i % H
+            if c == 0:
+                aa[i] = work.tile([P, N], BF16, name="aa", align_bytes=64)
+            cols = slice(CH * c, CH * (c + 1))
+            eng.tensor_tensor(out=aa[i][:, cols], in0=ex[i][:, cols], in1=gain[:, h, cols], op=ALU.mult)
+
+        def turn(i, half):
+            words = aa[i][:].bitcast(F32)
+            tp[i, half] = tp_pool.tile([P, 2, 2, P], F32, name="turned")
+            for g in range(2):
+                for u in range(2):
+                    w0 = 256 * (2 * half + g)
+                    nc.tensor.transpose(tp[i, half][:, g, u, :], words[:, w0 + u : w0 + 256 : 2], ident[:])
+
+        def spread(i, half):
+            if half == 0:
+                at[i] = work.tile([P, NCH * P * 4], BF16, name="at", bufs=3, align_bytes=64)
+            dst = at[i][:].bitcast(F32)[:, 512 * half : 512 * (half + 1)]
+            nc.scalar.copy(
+                out=dst.rearrange("p (g r u) -> p g r u", g=2, u=2), in_=tp[i, half][:].rearrange("p g u r -> p g r u")
+            )
+
+        def codes_tile(i):
+            cod[i] = work.tile([P, NCH * P], U32, name="cod", bufs=3, align_bytes=64)
+            cos[i] = work.tile([P, NCH * P], U8, name="cos", bufs=3, align_bytes=64)
+
+        def quant(i, g0, g1):
+            nc.vector.quantize_mx(
+                out=cod[i][:, P * g0 : P * g1].bitcast(FP8X4),
+                scales=cos[i][:, P * g0 : P * g1],
+                in_=at[i][:, 4 * P * g0 : 4 * P * g1],
+            )
+
+        def pv_mm(i, g):
+            h = i % H
+            if g == 0:
+                if i == TILES - 1:
+                    pv[i] = sc_pool.tile([P, D], F32, name="scores")
+                else:
+                    pv[i] = pv_pool.tile([P, D], F32, name="pv")
+            nc.tensor.matmul_mx(
+                out=pv[i][:],
+                lhsT=cod[i][:, P * g : P * (g + 1)].bitcast(FP8X4),
+                lhsT_scale=cos[i][:, P * g : P * (g + 1)],
+                rhs=vw[:, h * NCH + g, :].bitcast(FP4X4),
+                rhs_scale=vsc[:, h * NCH + g, :],
+                start=(g == 0),
+                stop=(g == NCH - 1),
+            )
+
+        def recip(i):
+            rec[i] = work.tile([P, 1], F32, name="rec", bufs=3)
+            nc.vector.reciprocal(out=rec[i][:], in_=tot[i][:])
+
+        def finish(i):
+            j, h = divmod(i, H)
+            cols = slice(h * D, (h + 1) * D)
+            res = work.tile([P, D], F32, name="res", bufs=3)
+            nc.vector.scalar_tensor_tensor(
+                out=res[:], in0=pv[i][:], scalar=rec[i][:], in1=sg[j][:, cols], op0=ALU.mult, op1=ALU.mult
+            )
+            nc.sync.dma_start(out=out[j * P : (j + 1) * P, cols], in_=res[:])
+
+        def x_part_turn(j, h, pool, name):
+            part = pool.tile([P, 2, P], F32, name=name)
+            words = xs[j][:].bitcast(F32)
+            for u in range(2):
+                nc.tensor.transpose(part[:, u, :], words[:, 256 * h + u : 256 * (h + 1) : 2], ident[:])
+            return part
+
+        def x_part_spread(h, part):
+            nc.scalar.copy(
+                out=xi0[:, h].rearrange("p r t -> p (r t)").bitcast(F32).rearrange("p (r u) -> p r u", u=2),
+                in_=part[:].rearrange("p u r -> p r u"),
+            )
+
+        def x_part_quant(h):
+            nc.vector.quantize_mx(
+                out=xcodes[:, 0, h * P : (h + 1) * P].bitcast(FP8X4),
+                scales=xqs[:, 0, h * P : (h + 1) * P],
+                in_=xi0[:, h].rearrange("p r t -> p (r t)"),
+            )
+
+        x_tile(0)
+        x_tile(1)
+        xi0 = work.tile([P, H, P, 4], BF16, name="x_spread", align_bytes=64)
+        x_scale_v(0, 0)
+        part0 = x_part_turn(0, 0, xt_pool, "x_turned")
+        x_scale_v(0, 1)
+        part1 = x_part_turn(0, 1, tp_pool, "turned")
+        x_scale_v(1, 0)
+        x_part_spread(0, part0)
+        x_part_quant(0)
+        for c in range(NCH):
+            qk(0, c)
+        x_part_spread(1, part1)
+        x_part_quant(1)
+        nc.vector.tensor_scalar_mul(nslope[:], slope[:], -1.0)
+        x_widen(2)
+        x_widen(3)
+
+        widen_at = {}
+        scale_at = {}
+        turn_at = {0: 2, 1: 3}
+        spread_at = {1: 2, 2: 3}
+        quant_at = {2: 2, 3: 3}
+        for j in range(4, QT):
+            widen_at[2 * j - 6] = j
+            scale_at[2 * j - 6] = (j, 0)
+            scale_at[2 * j - 5] = (j, 1)
+            turn_at[2 * j - 4] = j
+            spread_at[2 * j - 3] = j
+            quant_at[2 * j - 2] = j
+        tanh_at = {2 * j + 1: j for j in range(QT - 1)}
+        affine_at = {2 * j + 2: j for j in range(QT - 1)}
+        tanh_at[14] = 7
+        affine_at[15] = 7
+
+        for i in range(TILES):
+            last = i == TILES - 1
+            for c in range(NCH):
+                add_bias(i, c)
+                if not last:
+                    qk(i + 1, c)
+            if i == 0:
+                x_scale_v(1, 1)
+                x_turn(1)
+                x_spread(1)
+                for j in range(2, 4):
+                    x_scale_g(j, 0)
+                    x_scale_g(j, 1)
+            if i in spread_at:
+                x_spread(spread_at[i])
+            if i in affine_at:
+                gate_affine(affine_at[i])
+            if i in tanh_at:
+                gate_tanh(tanh_at[i])
+            if i in widen_at:
+                x_widen(widen_at[i])
+            if i >= 2:
+                turn(i - 2, 0)
+                turn(i - 2, 1)
+                spread(i - 2, 0)
+                spread(i - 2, 1)
+            if i >= 4:
+                finish(i - 4)
+            if i >= 4:
+                codes_tile(i - 3)
+                quant(i - 3, 0, NCH)
+                for g in range(NCH):
+                    pv_mm(i - 3, g)
+            if i in quant_at:
+                x_quant(quant_at[i])
+            if i >= 3:
+                recip(i - 3)
+            row_max(i)
+            if i == 3:
+                codes_tile(0)
+                quant(0, 0, NCH)
+                for g in range(NCH):
+                    pv_mm(0, g)
+            if i == 0:
+                x_quant(1)
+            if i in turn_at:
+                x_turn(turn_at[i])
+            if not last:
+                exps(i)
+                for c in range(NCH):
+                    gains(nc.gpsimd, i, c)
+                if i in scale_at:
+                    x_scale_g(*scale_at[i])
+
+        i = TILES - 1
+        exps_piece(i, 0)
+        finish(i - 3)
+        codes_tile(i - 2)
+        quant(i - 2, 0, NCH)
+        for g in range(NCH):
+            pv_mm(i - 2, g)
+        recip(i - 2)
+        gains(nc.vector, i, 0)
+        turn(i - 1, 0)
+        turn(i - 1, 1)
+        exps_piece(i, 1)
+        gains(nc.gpsimd, i, 1)
+        spread(i - 1, 0)
+        exps_piece(i, 2)
+        gains(nc.vector, i, 2)
+        finish(i - 2)
+        spread(i - 1, 1)
+        exps_piece(i, 3)
+        gains(nc.vector, i, 3)
+        turn(i, 0)
+        spread(i, 0)
+        recip(i - 1)
+        codes_tile(i - 1)
+        quant(i - 1, 0, NCH)
+        for g in range(NCH):
+            pv_mm(i - 1, g)
+        turn(i, 1)
+        tot[i] = work.tile([P, 1], F32, name="tot", bufs=5)
+        nc.vector.tensor_reduce(out=tot[i][:], in_=tot4[:], axis=AX.X, op=ALU.add)
+        spread(i, 1)
+        codes_tile(i)
+        quant(i, 0, 2)
+        for g in range(2):
+            pv_mm(i, g)
+        recip(i)
+        quant(i, 2, 4)
+        for g in range(2, 4):
+            pv_mm(i, g)
+        finish(i - 1)
+        finish(i)

@@ -180,7 +180,10 @@ def tile_alibi_slot_attention_f1_kernel(
 
         def row_max(i):
             nmx[i] = work.tile([P, 1], F32, name="nmx", bufs=3)
-            nc.vector.tensor_reduce(out=nmx[i][:], in_=neg[i][:], axis=AX.X, op=ALU.min)
+            scrap = work.tile([P, N], BF16, name="scrap", bufs=1)
+            nc.vector.tensor_scalar(
+                out=scrap[:], in0=neg[i][:], scalar1=1.0, scalar2=None, op0=ALU.mult, op1=ALU.min, accum_out=nmx[i][:]
+            )
 
         def exps(i):
             ex[i] = work.tile([P, N], F32, name="ex")

@@ -39,7 +39,7 @@ def tile_alibi_slot_attention_f1_kernel(
         ctx.enter_context(tc.manual_schedule())
 
         xb = keep.tile([P, QT, H * D], U8, name="xb", align_bytes=64)
-        xsc = keep.tile([P, H * D], F32, name="xsc")
+        xsc = keep.tile([P, H * 4], F32, name="xsc")
         kw = keep.tile([P, H, 2 * N], U8, name="kw", align_bytes=64)
         ksc = keep.tile([P, H, N], U8, name="ksc", align_bytes=64)
         vw = keep.tile([P, H * NCH, 2 * D], U8, name="vw", align_bytes=64)
@@ -64,7 +64,7 @@ def tile_alibi_slot_attention_f1_kernel(
         x_rows = x_bytes.rearrange("(j p) k -> p j k", p=P)
         bias_rows = bias.rearrange("(j p) n -> p j n", p=P)
         gate_rows = gate.rearrange("(j p) n -> p j n", p=P)
-        xs_row = x_scale.rearrange("o k -> (o k)")
+        xs_cols = x_scale.rearrange("o (h p t) -> p (o h) t", h=H, t=4)
         ks_i32 = k_scales.bitcast(I32).rearrange("g r n -> r g n")
         vs_i32 = v_scales.bitcast(I32).rearrange("g r n -> r g n")
         kw_rows = k_words.rearrange("g p n -> p g n")
@@ -74,8 +74,7 @@ def tile_alibi_slot_attention_f1_kernel(
             nc.sync.dma_start(out=dst, in_=src)
 
         load(xb[:, 0:2, :], x_rows[:, 0:2, :])
-        for h in range(H):
-            load(xsc[:, h * D : (h + 1) * D], xs_row[h * D : (h + 1) * D].partition_broadcast(P))
+        load(xsc[:].rearrange("p (h t) -> p h t", h=H), xs_cols)
         for q in range(4):
             load(ksc[32 * q : 32 * q + 4, :, :].bitcast(I32), ks_i32[4 * q : 4 * q + 4])
         load(kw[:, 0, 0:N], kw_rows[:, 0, 0:N])
@@ -102,45 +101,40 @@ def tile_alibi_slot_attention_f1_kernel(
             if j == 4:
                 load(gate_sb[:, 4:8, :], gate_rows[:, 4:8, :])
 
-        xw = {}
-        xs = {}
+        xc = {}
         xt = {}
+        xi = {}
 
-        def x_tile(j):
-            xs[j] = work.tile([P, H * D], BF16, name="x_scaled", bufs=3, align_bytes=64)
+        def x_cast(eng, j, h0, h1):
+            if h0 == 0:
+                xc[j] = work.tile([P, H * D], BF16, name="x_cast", bufs=3, align_bytes=64)
+            src = xb[:, j, h0 * D : h1 * D].bitcast(FP8)
+            if eng == "scalar":
+                nc.scalar.copy(out=xc[j][:, h0 * D : h1 * D], in_=src)
+            else:
+                nc.vector.tensor_copy(out=xc[j][:, h0 * D : h1 * D], in_=src)
 
-        def x_scale_v(j, h):
-            cols = slice(h * D, (h + 1) * D)
-            nc.vector.tensor_tensor(out=xs[j][:, cols], in0=xb[:, j, cols].bitcast(FP8), in1=xsc[:, cols], op=ALU.mult)
+        def x_turn(j, h, bank, pos):
+            words = xc[j][:].bitcast(F32)
+            for u in range(2):
+                nc.tensor.transpose(bank[:, pos, u, :], words[:, 256 * h + u : 256 * (h + 1) : 2], ident[:])
+            xt[j, h] = bank[:, pos, :, :].rearrange("p u r -> p (u r)").bitcast(BF16)
 
-        def x_widen(j):
-            xw[j] = work.tile([P, H * D], F32, name="x_wide")
-            nc.scalar.copy(out=xw[j][:], in_=xb[:, j, :].bitcast(FP8))
-
-        def x_scale_g(j, h):
+        def x_scale(j, h):
             if h == 0:
-                x_tile(j)
-            cols = slice(h * D, (h + 1) * D)
-            nc.gpsimd.tensor_tensor(out=xs[j][:, cols], in0=xw[j][:, cols], in1=xsc[:, cols], op=ALU.mult)
-
-        def x_turn(j):
-            words = xs[j][:].bitcast(F32)
-            xt[j] = xt_pool.tile([P, H, 2, P], F32, name="x_turned")
-            for h in range(H):
-                for u in range(2):
-                    nc.tensor.transpose(xt[j][:, h, u, :], words[:, 256 * h + u : 256 * (h + 1) : 2], ident[:])
-
-        def x_spread(j):
-            xi = work.tile([P, H, P, 4], BF16, name="x_spread", align_bytes=64)
-            nc.scalar.copy(
-                out=xi[:].rearrange("p h r t -> p (h r t)").bitcast(F32).rearrange("p (h r u) -> p h r u", h=H, u=2),
-                in_=xt[j][:].rearrange("p h u r -> p h r u"),
+                xi[j] = work.tile([P, H, P, 4], BF16, name="x_spread", align_bytes=64)
+            nc.vector.tensor_tensor(
+                out=xi[j][:, h].rearrange("p r (u e) -> p r u e", u=2),
+                in0=xt[j, h].rearrange("p (u r e) -> p r u e", u=2, e=2),
+                in1=xsc[:, 4 * h : 4 * h + 4].rearrange("p (u e) -> p u e", u=2).unsqueeze(1).broadcast_to([P, P, 2, 2]),
+                op=ALU.mult,
             )
-            xt[j] = xi
 
-        def x_quant(j):
+        def x_quant(j, h0, h1):
             nc.vector.quantize_mx(
-                out=xcodes[:, j, :].bitcast(FP8X4), scales=xqs[:, j, :], in_=xt[j][:].rearrange("p h r t -> p (h r t)")
+                out=xcodes[:, j, h0 * P : h1 * P].bitcast(FP8X4),
+                scales=xqs[:, j, h0 * P : h1 * P],
+                in_=xi[j][:, h0:h1].rearrange("p h r t -> p (h r t)"),
             )
 
         sg = {}
@@ -201,11 +195,11 @@ def tile_alibi_slot_attention_f1_kernel(
                 accum_out=tot4[:, c : c + 1],
             )
 
-        def gains(eng, i, c):
+        def gains(eng, i, c0, c1):
             h = i % H
-            if c == 0:
+            if c0 == 0:
                 aa[i] = work.tile([P, N], BF16, name="aa", align_bytes=64)
-            cols = slice(CH * c, CH * (c + 1))
+            cols = slice(CH * c0, CH * c1)
             eng.tensor_tensor(out=aa[i][:, cols], in0=ex[i][:, cols], in1=gain[:, h, cols], op=ALU.mult)
 
         def turn(i, half):
@@ -265,55 +259,34 @@ def tile_alibi_slot_attention_f1_kernel(
             )
             nc.sync.dma_start(out=out[j * P : (j + 1) * P, cols], in_=res[:])
 
-        def x_part_turn(j, h, pool, name):
-            part = pool.tile([P, 2, P], F32, name=name)
-            words = xs[j][:].bitcast(F32)
-            for u in range(2):
-                nc.tensor.transpose(part[:, u, :], words[:, 256 * h + u : 256 * (h + 1) : 2], ident[:])
-            return part
-
-        def x_part_spread(h, part):
-            nc.scalar.copy(
-                out=xi0[:, h].rearrange("p r t -> p (r t)").bitcast(F32).rearrange("p (r u) -> p r u", u=2),
-                in_=part[:].rearrange("p u r -> p r u"),
-            )
-
-        def x_part_quant(h):
-            nc.vector.quantize_mx(
-                out=xcodes[:, 0, h * P : (h + 1) * P].bitcast(FP8X4),
-                scales=xqs[:, 0, h * P : (h + 1) * P],
-                in_=xi0[:, h].rearrange("p r t -> p (r t)"),
-            )
-
-        x_tile(0)
-        x_tile(1)
-        xi0 = work.tile([P, H, P, 4], BF16, name="x_spread", align_bytes=64)
-        x_scale_v(0, 0)
-        part0 = x_part_turn(0, 0, xt_pool, "x_turned")
-        x_scale_v(0, 1)
-        part1 = x_part_turn(0, 1, tp_pool, "turned")
-        x_scale_v(1, 0)
-        x_part_spread(0, part0)
-        x_part_quant(0)
+        x_cast("vector", 0, 0, 1)
+        x_cast("scalar", 0, 1, 2)
+        bank0 = xt_pool.tile([P, 1, 2, P], F32, name="x_turned")
+        x_turn(0, 0, bank0, 0)
+        bank1 = tp_pool.tile([P, 1, 2, P], F32, name="turned")
+        x_turn(0, 1, bank1, 0)
+        x_cast("scalar", 1, 0, 2)
+        bank2 = tp_pool.tile([P, H, 2, P], F32, name="turned")
+        x_scale(0, 0)
+        x_turn(1, 0, bank2, 0)
+        x_turn(1, 1, bank2, 1)
+        x_scale(0, 1)
+        x_quant(0, 0, 1)
         for c in range(NCH):
             qk(0, c)
-        x_part_spread(1, part1)
-        x_part_quant(1)
+        x_scale(1, 0)
+        x_quant(0, 1, 2)
+        x_scale(1, 1)
         nc.vector.tensor_scalar_mul(nslope[:], slope[:], -1.0)
-        x_widen(2)
-        x_widen(3)
+        x_quant(1, 0, 2)
+        x_cast("scalar", 2, 0, 2)
 
-        widen_at = {}
-        scale_at = {}
-        turn_at = {0: 2, 1: 3}
-        spread_at = {1: 2, 2: 3}
-        quant_at = {2: 2, 3: 3}
-        for j in range(4, QT):
-            widen_at[2 * j - 6] = j
-            scale_at[2 * j - 6] = (j, 0)
-            scale_at[2 * j - 5] = (j, 1)
-            turn_at[2 * j - 4] = j
-            spread_at[2 * j - 3] = j
+        cast_at, turn_at, scale_at, quant_at = {}, {}, {}, {}
+        for j in range(2, QT):
+            if j > 2:
+                cast_at[2 * j - 5] = j
+            turn_at[2 * j - 4 if j > 2 else 0] = j
+            scale_at[2 * j - 3] = j
             quant_at[2 * j - 2] = j
         tanh_at = {2 * j + 1: j for j in range(QT - 1)}
         affine_at = {2 * j + 2: j for j in range(QT - 1)}
@@ -326,92 +299,81 @@ def tile_alibi_slot_attention_f1_kernel(
                 add_bias(i, c)
                 if not last:
                     qk(i + 1, c)
-            if i == 0:
-                x_scale_v(1, 1)
-                x_turn(1)
-                x_spread(1)
-                for j in range(2, 4):
-                    x_scale_g(j, 0)
-                    x_scale_g(j, 1)
-            if i in spread_at:
-                x_spread(spread_at[i])
+                if c == 0 and i == 4:
+                    codes_tile(0)
+                    quant(0, 0, NCH)
+                if c == (1 if i == 4 else 0) and i in quant_at:
+                    x_quant(quant_at[i], 0, 2)
+                if c == 2 and i >= 4:
+                    codes_tile(i - 3)
+                    quant(i - 3, 0, NCH)
             if i in affine_at:
                 gate_affine(affine_at[i])
             if i in tanh_at:
                 gate_tanh(tanh_at[i])
-            if i in widen_at:
-                x_widen(widen_at[i])
+            if i in cast_at:
+                x_cast("scalar", cast_at[i], 0, 2)
             if i >= 2:
-                turn(i - 2, 0)
-                turn(i - 2, 1)
-                spread(i - 2, 0)
-                spread(i - 2, 1)
-            if i >= 4:
-                finish(i - 4)
-            if i >= 4:
-                codes_tile(i - 3)
-                quant(i - 3, 0, NCH)
-                for g in range(NCH):
-                    pv_mm(i - 3, g)
-            if i in quant_at:
-                x_quant(quant_at[i])
-            if i >= 3:
-                recip(i - 3)
-            row_max(i)
-            if i == 3:
-                codes_tile(0)
-                quant(0, 0, NCH)
+                for half in range(2):
+                    turn(i - 2, half)
+                    spread(i - 2, half)
+            if i == 4:
                 for g in range(NCH):
                     pv_mm(0, g)
-            if i == 0:
-                x_quant(1)
+            if i >= 4:
+                finish(i - 4)
+                for g in range(NCH):
+                    pv_mm(i - 3, g)
+            if i >= 3:
+                recip(i - 3)
+            if i in scale_at:
+                x_scale(scale_at[i], 0)
+                x_scale(scale_at[i], 1)
+            row_max(i)
             if i in turn_at:
-                x_turn(turn_at[i])
+                jx = turn_at[i]
+                bank = xt_pool.tile([P, H, 2, P], F32, name="x_turned")
+                for h in range(H):
+                    x_turn(jx, h, bank, h)
             if not last:
                 exps(i)
-                for c in range(NCH):
-                    gains(nc.gpsimd, i, c)
-                if i in scale_at:
-                    x_scale_g(*scale_at[i])
+                for c in range(0, NCH, 2):
+                    gains(nc.gpsimd, i, c, c + 2)
 
         i = TILES - 1
-        exps_piece(i, 0)
+        for c in range(NCH):
+            exps_piece(i, c)
         finish(i - 3)
+        turn(i - 1, 0)
+        spread(i - 1, 0)
+        turn(i - 1, 1)
+        spread(i - 1, 1)
+        gains(nc.vector, i, 0, 1)
         codes_tile(i - 2)
         quant(i - 2, 0, NCH)
         for g in range(NCH):
             pv_mm(i - 2, g)
         recip(i - 2)
-        gains(nc.vector, i, 0)
-        turn(i - 1, 0)
-        turn(i - 1, 1)
-        exps_piece(i, 1)
-        gains(nc.gpsimd, i, 1)
-        spread(i - 1, 0)
-        exps_piece(i, 2)
-        gains(nc.vector, i, 2)
-        finish(i - 2)
-        spread(i - 1, 1)
-        exps_piece(i, 3)
-        gains(nc.vector, i, 3)
+        for c in range(1, NCH):
+            gains(nc.vector, i, c, c + 1)
         turn(i, 0)
         spread(i, 0)
-        recip(i - 1)
+        turn(i, 1)
+        spread(i, 1)
+        finish(i - 2)
         codes_tile(i - 1)
         quant(i - 1, 0, NCH)
         for g in range(NCH):
             pv_mm(i - 1, g)
-        turn(i, 1)
+        recip(i - 1)
         tot[i] = work.tile([P, 1], F32, name="tot", bufs=5)
         nc.vector.tensor_reduce(out=tot[i][:], in_=tot4[:], axis=AX.X, op=ALU.add)
-        spread(i, 1)
         codes_tile(i)
-        quant(i, 0, 2)
-        for g in range(2):
-            pv_mm(i, g)
-        recip(i)
-        quant(i, 2, 4)
-        for g in range(2, 4):
-            pv_mm(i, g)
+        for half in range(2):
+            quant(i, 2 * half, 2 * half + 2)
+            for g in range(2 * half, 2 * half + 2):
+                pv_mm(i, g)
+            if half == 0:
+                recip(i)
         finish(i - 1)
         finish(i)

@@ -78,28 +78,28 @@ def tile_alibi_slot_attention_f1_kernel(
         for q in range(4):
             load(ksc[32 * q : 32 * q + 4, :, :].bitcast(I32), ks_i32[4 * q : 4 * q + 4])
         load(kw[:, 0, 0:N], kw_rows[:, 0, 0:N])
-        load(kw[:, 0, N:], kw_rows[:, 0, N:])
-        load(slope[:], slopes.partition_broadcast(P))
         load(bias_sb[:, 0, 0 : N // 2], bias_rows[:, 0, 0 : N // 2])
+        load(slope[:], slopes.partition_broadcast(P))
+        load(kw[:, 0, N:], kw_rows[:, 0, N:])
         load(bias_sb[:, 0, N // 2 :], bias_rows[:, 0, N // 2 :])
+        load(gate_sb[:, 0, :], gate_rows[:, 0, :])
         load(xb[:, 2:4, :], x_rows[:, 2:4, :])
         load(kw[:, 1, :], kw_rows[:, 1, :])
         load(gain[:, 0, :], slot_gain[0, :].partition_broadcast(P))
-        load(gate_sb[:, 0, :], gate_rows[:, 0, :])
-        load(gate_sb[:, 1, :], gate_rows[:, 1, :])
-        load(gain[:, 1, :], slot_gain[1, :].partition_broadcast(P))
+        load(gate_sb[:, 1:3, :], gate_rows[:, 1:3, :])
         load(bias_sb[:, 1, :], bias_rows[:, 1, :])
+        load(gain[:, 1, :], slot_gain[1, :].partition_broadcast(P))
         for q in range(4):
             load(vsc[32 * q : 32 * q + 4, :, :].bitcast(I32), vs_i32[4 * q : 4 * q + 4])
         load(vw[:, 0:4, :], vw_rows[:, 0:4, :])
-        load(bias_sb[:, 2, :], bias_rows[:, 2, :])
         load(xb[:, 4:8, :], x_rows[:, 4:8, :])
+        load(bias_sb[:, 2, :], bias_rows[:, 2, :])
         load(vw[:, 4:8, :], vw_rows[:, 4:8, :])
-        load(gate_sb[:, 2:4, :], gate_rows[:, 2:4, :])
+        load(gate_sb[:, 3:5, :], gate_rows[:, 3:5, :])
         for j in range(3, QT):
             load(bias_sb[:, j, :], bias_rows[:, j, :])
             if j == 4:
-                load(gate_sb[:, 4:8, :], gate_rows[:, 4:8, :])
+                load(gate_sb[:, 5:8, :], gate_rows[:, 5:8, :])
 
         xc = {}
         xt = {}
@@ -130,6 +130,16 @@ def tile_alibi_slot_attention_f1_kernel(
                 op=ALU.mult,
             )
 
+        def x_scale_s(j, h):
+            if h == 0:
+                xi[j] = work.tile([P, H, P, 4], BF16, name="x_spread", align_bytes=64)
+            turned = xt[j, h].rearrange("p (u r e) -> p u r e", u=2, e=2)
+            for t in range(4):
+                nc.scalar.activation(
+                    out=xi[j][:, h, :, t], in_=turned[:, t // 2, :, t % 2], func=ACT.Copy,
+                    scale=xsc[:, 4 * h + t : 4 * h + t + 1],
+                )
+
         def x_quant(j, h0, h1):
             nc.vector.quantize_mx(
                 out=xcodes[:, j, h0 * P : h1 * P].bitcast(FP8X4),
@@ -142,6 +152,11 @@ def tile_alibi_slot_attention_f1_kernel(
         def gate_tanh(j):
             sg[j] = work.tile([P, H * D], F32, name="sgm", bufs=5)
             nc.scalar.activation(out=sg[j][:], in_=gate_sb[:, j, :], func=ACT.Tanh, scale=0.5)
+
+        def gate_affine_g(j):
+            nc.gpsimd.tensor_scalar(
+                out=sg[j][:], in0=sg[j][:], scalar1=0.5, scalar2=0.5, op0=ALU.mult, op1=ALU.add
+            )
 
         def gate_affine(j):
             nc.scalar.activation(out=sg[j][:], in_=sg[j][:], func=ACT.Copy, scale=0.5, bias=0.5)
@@ -173,7 +188,7 @@ def tile_alibi_slot_attention_f1_kernel(
             )
 
         def row_max(i):
-            nmx[i] = work.tile([P, 1], F32, name="nmx", bufs=3)
+            nmx[i] = work.tile([P, 1], F32, name="nmx", bufs=TILES)
             scrap = work.tile([P, N], BF16, name="scrap", bufs=1)
             nc.vector.tensor_scalar(
                 out=scrap[:], in0=neg[i][:], scalar1=1.0, scalar2=None, op0=ALU.mult, op1=ALU.min, accum_out=nmx[i][:]
@@ -181,9 +196,11 @@ def tile_alibi_slot_attention_f1_kernel(
 
         def exps(i):
             ex[i] = work.tile([P, N], F32, name="ex")
-            tot[i] = work.tile([P, 1], F32, name="tot", bufs=5)
+            j, h = divmod(i, H)
+            if h == 0:
+                tot[j] = work.tile([P, H], F32, name="tot", bufs=QT)
             nc.scalar.activation(
-                out=ex[i][:], in_=neg[i][:], func=ACT.Exp, bias=nmx[i][:], scale=-1.0, accum_out=tot[i][:]
+                out=ex[i][:], in_=neg[i][:], func=ACT.Exp, bias=nmx[i][:], scale=-1.0, accum_out=tot[j][:, h : h + 1]
             )
 
         def exps_piece(i, c):
@@ -246,16 +263,16 @@ def tile_alibi_slot_attention_f1_kernel(
                 stop=(g == NCH - 1),
             )
 
-        def recip(i):
-            rec[i] = work.tile([P, 1], F32, name="rec", bufs=3)
-            nc.vector.reciprocal(out=rec[i][:], in_=tot[i][:])
+        def recip(j):
+            rec[j] = work.tile([P, H], F32, name="rec", bufs=QT)
+            nc.vector.reciprocal(out=rec[j][:], in_=tot[j][:])
 
         def finish(i):
             j, h = divmod(i, H)
             cols = slice(h * D, (h + 1) * D)
-            res = work.tile([P, D], F32, name="res", bufs=3)
+            res = work.tile([P, D], F32, name="res", bufs=5)
             nc.vector.scalar_tensor_tensor(
-                out=res[:], in0=pv[i][:], scalar=rec[i][:], in1=sg[j][:, cols], op0=ALU.mult, op1=ALU.mult
+                out=res[:], in0=pv[i][:], scalar=rec[j][:, h : h + 1], in1=sg[j][:, cols], op0=ALU.mult, op1=ALU.mult
             )
             nc.sync.dma_start(out=out[j * P : (j + 1) * P, cols], in_=res[:])
 
@@ -274,24 +291,20 @@ def tile_alibi_slot_attention_f1_kernel(
         x_quant(0, 0, 1)
         for c in range(NCH):
             qk(0, c)
-        x_scale(1, 0)
-        x_quant(0, 1, 2)
-        x_scale(1, 1)
         nc.vector.tensor_scalar_mul(nslope[:], slope[:], -1.0)
-        x_quant(1, 0, 2)
+        x_quant(0, 1, 2)
+        x_scale_s(1, 0)
+        gate_tanh(0)
+        gate_affine_g(0)
         x_cast("scalar", 2, 0, 2)
 
-        cast_at, turn_at, scale_at, quant_at = {}, {}, {}, {}
-        for j in range(2, QT):
-            if j > 2:
-                cast_at[2 * j - 5] = j
-            turn_at[2 * j - 4 if j > 2 else 0] = j
-            scale_at[2 * j - 3] = j
-            quant_at[2 * j - 2] = j
-        tanh_at = {2 * j + 1: j for j in range(QT - 1)}
-        affine_at = {2 * j + 2: j for j in range(QT - 1)}
-        tanh_at[14] = 7
-        affine_at[15] = 7
+        cast_at = {1: 3, 4: 4, 5: 5, 8: 6, 9: 7}
+        turn_at = {0: 2, 1: 3, 4: 4, 5: 5, 8: 6, 9: 7}
+        scale_v_at = {1: 2, 5: 4, 9: 6}
+        scale_s_at = {2: (3, 0), 3: (3, 1), 6: (5, 0), 7: (5, 1), 10: (7, 0), 11: (7, 1)}
+        quant_at = {2: 2, 4: 3, 6: 4, 8: 5, 10: 6, 12: 7}
+        tanh_at = {1: 1, 4: 2, 5: 3, 9: 4, 12: 5, 13: 6, 14: 7}
+        affine_at = {1: 1, 5: 2, 8: 3, 9: 4, 12: 5, 13: 6, 15: 7}
 
         for i in range(TILES):
             last = i == TILES - 1
@@ -299,37 +312,38 @@ def tile_alibi_slot_attention_f1_kernel(
                 add_bias(i, c)
                 if not last:
                     qk(i + 1, c)
-                if c == 0 and i == 4:
-                    codes_tile(0)
-                    quant(0, 0, NCH)
-                if c == (1 if i == 4 else 0) and i in quant_at:
+                if c == 1 and i in quant_at:
                     x_quant(quant_at[i], 0, 2)
-                if c == 2 and i >= 4:
+                if c == (1 if i in quant_at else 2) and i >= 3:
                     codes_tile(i - 3)
                     quant(i - 3, 0, NCH)
-            if i in affine_at:
-                gate_affine(affine_at[i])
-            if i in tanh_at:
-                gate_tanh(tanh_at[i])
+            if i == 0:
+                x_scale(1, 1)
             if i in cast_at:
                 x_cast("scalar", cast_at[i], 0, 2)
+            if i in scale_s_at:
+                x_scale_s(*scale_s_at[i])
+            if i in tanh_at:
+                gate_tanh(tanh_at[i])
+            if i in affine_at:
+                gate_affine(affine_at[i])
             if i >= 2:
                 for half in range(2):
                     turn(i - 2, half)
                     spread(i - 2, half)
-            if i == 4:
-                for g in range(NCH):
-                    pv_mm(0, g)
             if i >= 4:
                 finish(i - 4)
+            if i >= 3:
                 for g in range(NCH):
                     pv_mm(i - 3, g)
-            if i >= 3:
-                recip(i - 3)
-            if i in scale_at:
-                x_scale(scale_at[i], 0)
-                x_scale(scale_at[i], 1)
+            if i in scale_v_at:
+                x_scale(scale_v_at[i], 0)
+                x_scale(scale_v_at[i], 1)
+            if i >= 3 and i % 2 == 1:
+                recip((i - 3) // 2)
             row_max(i)
+            if i == 0:
+                x_quant(1, 0, 2)
             if i in turn_at:
                 jx = turn_at[i]
                 bank = xt_pool.tile([P, H, 2, P], F32, name="x_turned")
@@ -353,7 +367,6 @@ def tile_alibi_slot_attention_f1_kernel(
         quant(i - 2, 0, NCH)
         for g in range(NCH):
             pv_mm(i - 2, g)
-        recip(i - 2)
         for c in range(1, NCH):
             gains(nc.vector, i, c, c + 1)
         turn(i, 0)
@@ -365,15 +378,13 @@ def tile_alibi_slot_attention_f1_kernel(
         quant(i - 1, 0, NCH)
         for g in range(NCH):
             pv_mm(i - 1, g)
-        recip(i - 1)
-        tot[i] = work.tile([P, 1], F32, name="tot", bufs=5)
-        nc.vector.tensor_reduce(out=tot[i][:], in_=tot4[:], axis=AX.X, op=ALU.add)
+        nc.vector.tensor_reduce(out=tot[QT - 1][:, H - 1 : H], in_=tot4[:], axis=AX.X, op=ALU.add)
         codes_tile(i)
         for half in range(2):
             quant(i, 2 * half, 2 * half + 2)
             for g in range(2 * half, 2 * half + 2):
                 pv_mm(i, g)
             if half == 0:
-                recip(i)
+                recip(QT - 1)
         finish(i - 1)
         finish(i)

@@ -73,13 +73,14 @@ def tile_alibi_slot_attention_f1_kernel(
         def load(dst, src):
             nc.sync.dma_start(out=dst, in_=src)
 
-        load(xb[:, 0:2, :], x_rows[:, 0:2, :])
+        load(xb[:, 0, :], x_rows[:, 0, :])
         load(xsc[:].rearrange("p (h t) -> p h t", h=H), xs_cols)
+        load(slope[:], slopes.partition_broadcast(P))
+        load(xb[:, 1, :], x_rows[:, 1, :])
         for q in range(4):
             load(ksc[32 * q : 32 * q + 4, :, :].bitcast(I32), ks_i32[4 * q : 4 * q + 4])
         load(kw[:, 0, 0:N], kw_rows[:, 0, 0:N])
         load(bias_sb[:, 0, 0 : N // 2], bias_rows[:, 0, 0 : N // 2])
-        load(slope[:], slopes.partition_broadcast(P))
         load(kw[:, 0, N:], kw_rows[:, 0, N:])
         load(bias_sb[:, 0, N // 2 :], bias_rows[:, 0, N // 2 :])
         load(gate_sb[:, 0, :], gate_rows[:, 0, :])
@@ -229,15 +230,15 @@ def tile_alibi_slot_attention_f1_kernel(
 
         def spread(i, half):
             if half == 0:
-                at[i] = work.tile([P, NCH * P * 4], BF16, name="at", bufs=3, align_bytes=64)
+                at[i] = work.tile([P, NCH * P * 4], BF16, name="at", bufs=2, align_bytes=64)
             dst = at[i][:].bitcast(F32)[:, 512 * half : 512 * (half + 1)]
             nc.scalar.copy(
                 out=dst.rearrange("p (g r u) -> p g r u", g=2, u=2), in_=tp[i, half][:].rearrange("p g u r -> p g r u")
             )
 
         def codes_tile(i):
-            cod[i] = work.tile([P, NCH * P], U32, name="cod", bufs=3, align_bytes=64)
-            cos[i] = work.tile([P, NCH * P], U8, name="cos", bufs=3, align_bytes=64)
+            cod[i] = work.tile([P, NCH * P], U32, name="cod", bufs=2, align_bytes=64)
+            cos[i] = work.tile([P, NCH * P], U8, name="cos", bufs=2, align_bytes=64)
 
         def quant(i, g0, g1):
             nc.vector.quantize_mx(
@@ -249,7 +250,7 @@ def tile_alibi_slot_attention_f1_kernel(
         def pv_mm(i, g):
             h = i % H
             if g == 0:
-                if i == TILES - 1:
+                if i >= TILES - 2:
                     pv[i] = sc_pool.tile([P, D], F32, name="scores")
                 else:
                     pv[i] = pv_pool.tile([P, D], F32, name="pv")
@@ -270,7 +271,7 @@ def tile_alibi_slot_attention_f1_kernel(
         def finish(i):
             j, h = divmod(i, H)
             cols = slice(h * D, (h + 1) * D)
-            res = work.tile([P, D], F32, name="res", bufs=5)
+            res = work.tile([P, D], F32, name="res", bufs=TILES)
             nc.vector.scalar_tensor_tensor(
                 out=res[:], in0=pv[i][:], scalar=rec[j][:, h : h + 1], in1=sg[j][:, cols], op0=ALU.mult, op1=ALU.mult
             )
@@ -283,17 +284,19 @@ def tile_alibi_slot_attention_f1_kernel(
         bank1 = tp_pool.tile([P, 1, 2, P], F32, name="turned")
         x_turn(0, 1, bank1, 0)
         x_cast("scalar", 1, 0, 2)
-        bank2 = tp_pool.tile([P, H, 2, P], F32, name="turned")
+        bank2 = tp_pool.tile([P, 1, 2, P], F32, name="turned")
+        nc.vector.tensor_scalar_mul(nslope[:], slope[:], -1.0)
         x_scale(0, 0)
         x_turn(1, 0, bank2, 0)
-        x_turn(1, 1, bank2, 1)
+        bank3 = xt_pool.tile([P, 1, 2, P], F32, name="x_turned")
+        x_turn(1, 1, bank3, 0)
         x_scale(0, 1)
         x_quant(0, 0, 1)
         for c in range(NCH):
             qk(0, c)
-        nc.vector.tensor_scalar_mul(nslope[:], slope[:], -1.0)
         x_quant(0, 1, 2)
         x_scale_s(1, 0)
+        x_scale(1, 1)
         gate_tanh(0)
         gate_affine_g(0)
         x_cast("scalar", 2, 0, 2)
@@ -312,13 +315,13 @@ def tile_alibi_slot_attention_f1_kernel(
                 add_bias(i, c)
                 if not last:
                     qk(i + 1, c)
-                if c == 1 and i in quant_at:
+                if c == 2 and i in quant_at:
                     x_quant(quant_at[i], 0, 2)
-                if c == (1 if i in quant_at else 2) and i >= 3:
+                if c == 2 and i >= 3:
                     codes_tile(i - 3)
                     quant(i - 3, 0, NCH)
             if i == 0:
-                x_scale(1, 1)
+                x_quant(1, 0, 2)
             if i in cast_at:
                 x_cast("scalar", cast_at[i], 0, 2)
             if i in scale_s_at:
@@ -342,8 +345,6 @@ def tile_alibi_slot_attention_f1_kernel(
             if i >= 3 and i % 2 == 1:
                 recip((i - 3) // 2)
             row_max(i)
-            if i == 0:
-                x_quant(1, 0, 2)
             if i in turn_at:
                 jx = turn_at[i]
                 bank = xt_pool.tile([P, H, 2, P], F32, name="x_turned")
@@ -351,13 +352,13 @@ def tile_alibi_slot_attention_f1_kernel(
                     x_turn(jx, h, bank, h)
             if not last:
                 exps(i)
-                for c in range(0, NCH, 2):
-                    gains(nc.gpsimd, i, c, c + 2)
+                gains(nc.gpsimd, i, 0, NCH if i < TILES - 2 else NCH - 1)
 
         i = TILES - 1
         for c in range(NCH):
             exps_piece(i, c)
         finish(i - 3)
+        gains(nc.vector, i - 1, NCH - 1, NCH)
         turn(i - 1, 0)
         spread(i - 1, 0)
         turn(i - 1, 1)
@@ -373,11 +374,11 @@ def tile_alibi_slot_attention_f1_kernel(
         spread(i, 0)
         turn(i, 1)
         spread(i, 1)
-        finish(i - 2)
         codes_tile(i - 1)
         quant(i - 1, 0, NCH)
         for g in range(NCH):
             pv_mm(i - 1, g)
+        finish(i - 2)
         nc.vector.tensor_reduce(out=tot[QT - 1][:, H - 1 : H], in_=tot4[:], axis=AX.X, op=ALU.add)
         codes_tile(i)
         for half in range(2):

from contextlib import ExitStack

import concourse.mybir as mybir
from concourse.masks import make_identity

F32 = mybir.dt.float32
BF16 = mybir.dt.bfloat16
I32 = mybir.dt.int32
U32 = mybir.dt.uint32
U8 = mybir.dt.uint8
FP8 = mybir.dt.float8_e4m3fn
FP8X4 = mybir.dt.float8_e4m3fn_x4
FP4X4 = mybir.dt.float4_e2m1fn_x4
ACT = mybir.ActivationFunctionType
ALU = mybir.AluOpType
AX = mybir.AxisListType

M, H, D, N = 1024, 2, 512, 2048
P = 128
QT = M // P
TILES = QT * H
CH = 512
NCH = N // CH

FLOPS = 2 * 2 * H * M * D * N


def tile_alibi_slot_attention_f1_kernel(
    tc, x_bytes, x_scale, k_words, k_scales, v_words, v_scales, bias, slopes, slot_gain, gate, out
):
    nc = tc.nc
    with ExitStack() as ctx:
        keep = ctx.enter_context(tc.tile_pool(name="keep", bufs=1))
        work = ctx.enter_context(tc.tile_pool(name="work", bufs=2))
        sc_pool = ctx.enter_context(tc.psum_pool(name="sc_pool", bufs=4))
        tp_pool = ctx.enter_context(tc.psum_pool(name="tp_pool", bufs=2))
        pv_pool = ctx.enter_context(tc.psum_pool(name="pv_pool", bufs=1))
        xt_pool = ctx.enter_context(tc.psum_pool(name="xt_pool", bufs=1))
        ctx.enter_context(tc.manual_schedule())

        xb = keep.tile([P, QT, H * D], U8, name="xb", align_bytes=64)
        xsc = keep.tile([P, H * 4], F32, name="xsc")
        kw = keep.tile([P, H, 2 * N], U8, name="kw", align_bytes=64)
        ksc = keep.tile([P, H, N], U8, name="ksc", align_bytes=64)
        vw = keep.tile([P, H * NCH, 2 * D], U8, name="vw", align_bytes=64)
        vsc = keep.tile([P, H * NCH, D], U8, name="vsc", align_bytes=64)
        bias_sb = keep.tile([P, QT, N], BF16, name="bias_sb")
        gain = keep.tile([P, H, N], BF16, name="gain")
        gate_sb = keep.tile([P, QT, H * D], BF16, name="gate_sb")
        slope = keep.tile([P, H], BF16, name="slope")
        nslope = keep.tile([P, H], F32, name="nslope")
        xcodes = keep.tile([P, QT, H * P], U32, name="xcodes", align_bytes=64)
        xqs = keep.tile([P, QT, H * P], U8, name="xqs", align_bytes=64)
        ident = keep.tile([P, P], F32, name="ident")
        dummy = keep.tile([P, 1], F32, name="dummy")
        tot4 = keep.tile([P, NCH], F32, name="tot4")

        nc.vector.memset(dummy[:], 0.0)
        nc.scalar.activation(out=dummy[:], in_=dummy[:], func=ACT.Exp)
        nc.vector.memset(ksc[:].rearrange("p g n -> p (g n)").bitcast(I32), 0)
        make_identity(nc, ident[:])
        nc.vector.memset(vsc[:].rearrange("p g n -> p (g n)").bitcast(I32), 0)

        x_rows = x_bytes.rearrange("(j p) k -> p j k", p=P)
        bias_rows = bias.rearrange("(j p) n -> p j n", p=P)
        gate_rows = gate.rearrange("(j p) n -> p j n", p=P)
        xs_cols = x_scale.rearrange("o (h p t) -> p (o h) t", h=H, t=4)
        ks_i32 = k_scales.bitcast(I32).rearrange("g r n -> r g n")
        vs_i32 = v_scales.bitcast(I32).rearrange("g r n -> r g n")
        kw_rows = k_words.rearrange("g p n -> p g n")
        vw_rows = v_words.rearrange("g p n -> p g n")

        def load(dst, src):
            nc.sync.dma_start(out=dst, in_=src)

        load(xb[:, 0, :], x_rows[:, 0, :])
        load(xsc[:].rearrange("p (h t) -> p h t", h=H), xs_cols)
        load(slope[:], slopes.partition_broadcast(P))
        load(xb[:, 1, :], x_rows[:, 1, :])
        for q in range(4):
            load(ksc[32 * q : 32 * q + 4, :, :].bitcast(I32), ks_i32[4 * q : 4 * q + 4])
        load(kw[:, 0, 0:N], kw_rows[:, 0, 0:N])
        load(bias_sb[:, 0, 0 : N // 2], bias_rows[:, 0, 0 : N // 2])
        load(kw[:, 0, N:], kw_rows[:, 0, N:])
        load(bias_sb[:, 0, N // 2 :], bias_rows[:, 0, N // 2 :])
        load(gate_sb[:, 0, :], gate_rows[:, 0, :])
        load(xb[:, 2:4, :], x_rows[:, 2:4, :])
        load(kw[:, 1, :], kw_rows[:, 1, :])
        load(gain[:, 0, :], slot_gain[0, :].partition_broadcast(P))
        load(gate_sb[:, 1:3, :], gate_rows[:, 1:3, :])
        load(bias_sb[:, 1, :], bias_rows[:, 1, :])
        load(gain[:, 1, :], slot_gain[1, :].partition_broadcast(P))
        for q in range(4):
            load(vsc[32 * q : 32 * q + 4, :, :].bitcast(I32), vs_i32[4 * q : 4 * q + 4])
        load(vw[:, 0:4, :], vw_rows[:, 0:4, :])
        load(xb[:, 4:8, :], x_rows[:, 4:8, :])
        load(bias_sb[:, 2, :], bias_rows[:, 2, :])
        load(vw[:, 4:8, :], vw_rows[:, 4:8, :])
        load(gate_sb[:, 3:5, :], gate_rows[:, 3:5, :])
        for j in range(3, QT):
            load(bias_sb[:, j, :], bias_rows[:, j, :])
            if j == 4:
                load(gate_sb[:, 5:8, :], gate_rows[:, 5:8, :])

        xc = {}
        xt = {}
        xi = {}

        def x_cast(eng, j, h0, h1):
            if h0 == 0:
                xc[j] = work.tile([P, H * D], BF16, name="x_cast", bufs=3, align_bytes=64)
            src = xb[:, j, h0 * D : h1 * D].bitcast(FP8)
            if eng == "scalar":
                nc.scalar.copy(out=xc[j][:, h0 * D : h1 * D], in_=src)
            else:
                nc.vector.tensor_copy(out=xc[j][:, h0 * D : h1 * D], in_=src)

        def x_turn(j, h, bank, pos):
            words = xc[j][:].bitcast(F32)
            for u in range(2):
                nc.tensor.transpose(bank[:, pos, u, :], words[:, 256 * h + u : 256 * (h + 1) : 2], ident[:])
            xt[j, h] = bank[:, pos, :, :].rearrange("p u r -> p (u r)").bitcast(BF16)

        def x_scale(j, h):
            if h == 0:
                xi[j] = work.tile([P, H, P, 4], BF16, name="x_spread", align_bytes=64)
            nc.vector.tensor_tensor(
                out=xi[j][:, h].rearrange("p r (u e) -> p r u e", u=2),
                in0=xt[j, h].rearrange("p (u r e) -> p r u e", u=2, e=2),
                in1=xsc[:, 4 * h : 4 * h + 4].rearrange("p (u e) -> p u e", u=2).unsqueeze(1).broadcast_to([P, P, 2, 2]),
                op=ALU.mult,
            )

        def x_scale_s(j, h):
            if h == 0:
                xi[j] = work.tile([P, H, P, 4], BF16, name="x_spread", align_bytes=64)
            turned = xt[j, h].rearrange("p (u r e) -> p u r e", u=2, e=2)
            for t in range(4):
                nc.scalar.activation(
                    out=xi[j][:, h, :, t], in_=turned[:, t // 2, :, t % 2], func=ACT.Copy,
                    scale=xsc[:, 4 * h + t : 4 * h + t + 1],
                )

        def x_quant(j, h0, h1):
            nc.vector.quantize_mx(
                out=xcodes[:, j, h0 * P : h1 * P].bitcast(FP8X4),
                scales=xqs[:, j, h0 * P : h1 * P],
                in_=xi[j][:, h0:h1].rearrange("p h r t -> p (h r t)"),
            )

        sg = {}

        def gate_tanh(j):
            sg[j] = work.tile([P, H * D], F32, name="sgm", bufs=5)
            nc.scalar.activation(out=sg[j][:], in_=gate_sb[:, j, :], func=ACT.Tanh, scale=0.5)

        def gate_affine_g(j):
            nc.gpsimd.tensor_scalar(
                out=sg[j][:], in0=sg[j][:], scalar1=0.5, scalar2=0.5, op0=ALU.mult, op1=ALU.add
            )

        def gate_affine(j):
            nc.scalar.activation(out=sg[j][:], in_=sg[j][:], func=ACT.Copy, scale=0.5, bias=0.5)

        sc, neg, nmx, ex, tot, aa = {}, {}, {}, {}, {}, {}
        tp, at, cod, cos, pv, rec = {}, {}, {}, {}, {}, {}

        def qk(i, c):
            j, h = divmod(i, H)
            sc[i, c] = sc_pool.tile([P, CH], F32, name="scores")
            nc.tensor.matmul_mx(
                out=sc[i, c][:],
                lhsT=xcodes[:, j, h * P : (h + 1) * P].bitcast(FP8X4),
                lhsT_scale=xqs[:, j, h * P : (h + 1) * P],
                rhs=kw[:, h, 2 * CH * c : 2 * CH * (c + 1)].bitcast(FP4X4),
                rhs_scale=ksc[:, h, CH * c : CH * (c + 1)],
                start=True,
                stop=True,
            )

        def add_bias(i, c):
            j, h = divmod(i, H)
            if c == 0:
                neg[i] = work.tile([P, N], F32, name="neg", bufs=3)
            cols = slice(CH * c, CH * (c + 1))
            nc.vector.scalar_tensor_tensor(
                out=neg[i][:, cols], in0=bias_sb[:, j, cols], scalar=nslope[:, h : h + 1], in1=sc[i, c][:],
                op0=ALU.mult, op1=ALU.subtract,
            )

        def row_max(i):
            nmx[i] = work.tile([P, 1], F32, name="nmx", bufs=TILES)
            scrap = work.tile([P, N], BF16, name="scrap", bufs=1)
            nc.vector.tensor_scalar(
                out=scrap[:], in0=neg[i][:], scalar1=1.0, scalar2=None, op0=ALU.mult, op1=ALU.min, accum_out=nmx[i][:]
            )

        def exps(i):
            ex[i] = work.tile([P, N], F32, name="ex")
            j, h = divmod(i, H)
            if h == 0:
                tot[j] = work.tile([P, H], F32, name="tot", bufs=QT)
            nc.scalar.activation(
                out=ex[i][:], in_=neg[i][:], func=ACT.Exp, bias=nmx[i][:], scale=-1.0, accum_out=tot[j][:, h : h + 1]
            )

        def exps_piece(i, c):
            if c == 0:
                ex[i] = work.tile([P, N], F32, name="ex")
            cols = slice(CH * c, CH * (c + 1))
            nc.scalar.activation(
                out=ex[i][:, cols], in_=neg[i][:, cols], func=ACT.Exp, bias=nmx[i][:], scale=-1.0,
                accum_out=tot4[:, c : c + 1],
            )

        def gains(eng, i, c0, c1):
            h = i % H
            if c0 == 0:
                aa[i] = work.tile([P, N], BF16, name="aa", align_bytes=64)
            cols = slice(CH * c0, CH * c1)
            eng.tensor_tensor(out=aa[i][:, cols], in0=ex[i][:, cols], in1=gain[:, h, cols], op=ALU.mult)

        def turn(i, half):
            words = aa[i][:].bitcast(F32)
            tp[i, half] = tp_pool.tile([P, 2, 2, P], F32, name="turned")
            for g in range(2):
                for u in range(2):
                    w0 = 256 * (2 * half + g)
                    nc.tensor.transpose(tp[i, half][:, g, u, :], words[:, w0 + u : w0 + 256 : 2], ident[:])

        def spread(i, half):
            if half == 0:
                at[i] = work.tile([P, NCH * P * 4], BF16, name="at", bufs=2, align_bytes=64)
            dst = at[i][:].bitcast(F32)[:, 512 * half : 512 * (half + 1)]
            nc.scalar.copy(
                out=dst.rearrange("p (g r u) -> p g r u", g=2, u=2), in_=tp[i, half][:].rearrange("p g u r -> p g r u")
            )

        def codes_tile(i):
            cod[i] = work.tile([P, NCH * P], U32, name="cod", bufs=2, align_bytes=64)
            cos[i] = work.tile([P, NCH * P], U8, name="cos", bufs=2, align_bytes=64)

        def quant(i, g0, g1):
            nc.vector.quantize_mx(
                out=cod[i][:, P * g0 : P * g1].bitcast(FP8X4),
                scales=cos[i][:, P * g0 : P * g1],
                in_=at[i][:, 4 * P * g0 : 4 * P * g1],
            )

        def pv_mm(i, g):
            h = i % H
            if g == 0:
                if i >= TILES - 2:
                    pv[i] = sc_pool.tile([P, D], F32, name="scores")
                else:
                    pv[i] = pv_pool.tile([P, D], F32, name="pv")
            nc.tensor.matmul_mx(
                out=pv[i][:],
                lhsT=cod[i][:, P * g : P * (g + 1)].bitcast(FP8X4),
                lhsT_scale=cos[i][:, P * g : P * (g + 1)],
                rhs=vw[:, h * NCH + g, :].bitcast(FP4X4),
                rhs_scale=vsc[:, h * NCH + g, :],
                start=(g == 0),
                stop=(g == NCH - 1),
            )

        def recip(j):
            rec[j] = work.tile([P, H], F32, name="rec", bufs=QT)
            nc.vector.reciprocal(out=rec[j][:], in_=tot[j][:])

        def finish(i):
            j, h = divmod(i, H)
            cols = slice(h * D, (h + 1) * D)
            res = work.tile([P, D], F32, name="res", bufs=TILES)
            nc.vector.scalar_tensor_tensor(
                out=res[:], in0=pv[i][:], scalar=rec[j][:, h : h + 1], in1=sg[j][:, cols], op0=ALU.mult, op1=ALU.mult
            )
            nc.sync.dma_start(out=out[j * P : (j + 1) * P, cols], in_=res[:])

        x_cast("vector", 0, 0, 1)
        x_cast("scalar", 0, 1, 2)
        bank0 = xt_pool.tile([P, 1, 2, P], F32, name="x_turned")
        x_turn(0, 0, bank0, 0)
        bank1 = tp_pool.tile([P, 1, 2, P], F32, name="turned")
        x_turn(0, 1, bank1, 0)
        x_cast("scalar", 1, 0, 2)
        bank2 = tp_pool.tile([P, 1, 2, P], F32, name="turned")
        nc.vector.tensor_scalar_mul(nslope[:], slope[:], -1.0)
        x_scale(0, 0)
        x_turn(1, 0, bank2, 0)
        bank3 = xt_pool.tile([P, 1, 2, P], F32, name="x_turned")
        x_turn(1, 1, bank3, 0)
        x_scale(0, 1)
        x_quant(0, 0, 1)
        for c in range(NCH):
            qk(0, c)
        x_quant(0, 1, 2)
        x_scale_s(1, 0)
        x_scale(1, 1)
        gate_tanh(0)
        gate_affine_g(0)
        x_cast("scalar", 2, 0, 2)

        cast_at = {1: 3, 4: 4, 5: 5, 8: 6, 9: 7}
        turn_at = {0: 2, 1: 3, 4: 4, 5: 5, 8: 6, 9: 7}
        scale_v_at = {1: 2, 5: 4, 9: 6}
        scale_s_at = {2: (3, 0), 3: (3, 1), 6: (5, 0), 7: (5, 1), 10: (7, 0), 11: (7, 1)}
        quant_at = {2: 2, 4: 3, 6: 4, 8: 5, 10: 6, 12: 7}
        tanh_at = {1: 1, 4: 2, 5: 3, 9: 4, 12: 5, 13: 6, 14: 7}
        affine_at = {1: 1, 5: 2, 8: 3, 9: 4, 12: 5, 13: 6, 15: 7}

        for i in range(TILES):
            last = i == TILES - 1
            for c in range(NCH):
                add_bias(i, c)
                if not last:
                    qk(i + 1, c)
                if c == 2 and i in quant_at:
                    x_quant(quant_at[i], 0, 2)
                if c == 2 and i >= 3:
                    codes_tile(i - 3)
                    quant(i - 3, 0, NCH)
            if i == 0:
                x_quant(1, 0, 2)
            if i in cast_at:
                x_cast("scalar", cast_at[i], 0, 2)
            if i in scale_s_at:
                x_scale_s(*scale_s_at[i])
            if i in tanh_at:
                gate_tanh(tanh_at[i])
            if i in affine_at:
                gate_affine(affine_at[i])
            if i >= 2:
                for half in range(2):
                    turn(i - 2, half)
                    spread(i - 2, half)
            if i >= 4:
                finish(i - 4)
            if i >= 3:
                for g in range(NCH):
                    pv_mm(i - 3, g)
            if i in scale_v_at:
                x_scale(scale_v_at[i], 0)
                x_scale(scale_v_at[i], 1)
            if i >= 3 and i % 2 == 1:
                recip((i - 3) // 2)
            row_max(i)
            if i in turn_at:
                jx = turn_at[i]
                bank = xt_pool.tile([P, H, 2, P], F32, name="x_turned")
                for h in range(H):
                    x_turn(jx, h, bank, h)
            if not last:
                exps(i)
                gains(nc.gpsimd, i, 0, NCH if i < TILES - 2 else NCH - 1)

        i = TILES - 1
        for c in range(NCH):
            exps_piece(i, c)
        finish(i - 3)
        gains(nc.vector, i - 1, NCH - 1, NCH)
        turn(i - 1, 0)
        spread(i - 1, 0)
        turn(i - 1, 1)
        spread(i - 1, 1)
        gains(nc.vector, i, 0, 1)
        codes_tile(i - 2)
        quant(i - 2, 0, NCH)
        for g in range(NCH):
            pv_mm(i - 2, g)
        for c in range(1, NCH):
            gains(nc.vector, i, c, c + 1)
        turn(i, 0)
        spread(i, 0)
        turn(i, 1)
        spread(i, 1)
        codes_tile(i - 1)
        quant(i - 1, 0, NCH)
        for g in range(NCH):
            pv_mm(i - 1, g)
        finish(i - 2)
        nc.vector.tensor_reduce(out=tot[QT - 1][:, H - 1 : H], in_=tot4[:], axis=AX.X, op=ALU.add)
        codes_tile(i)
        for half in range(2):
            quant(i, 2 * half, 2 * half + 2)
            for g in range(2 * half, 2 * half + 2):
                pv_mm(i, g)
            if half == 0:
                recip(QT - 1)
        finish(i - 1)
        finish(i)
